import numpy as np
import ml_dtypes


def mxq(x, axis, fmt="e4m3"):
    dtype, down = {"e4m3": (ml_dtypes.float8_e4m3fn, 7), "e5m2": (ml_dtypes.float8_e5m2, 14)}[fmt]
    v = np.moveaxis(np.asarray(x, np.float32).astype(ml_dtypes.bfloat16).astype(np.float64), axis, -1)
    blocks = v.reshape(v.shape[:-1] + (-1, 32))
    amax = np.abs(blocks).max(-1, keepdims=True)
    byte = np.maximum(np.where(amax > 0, np.frexp(amax)[1] - 1 + 127, 0) - down, 1)
    scale = np.exp2(byte - 127.0)
    codes = (blocks / scale).astype(np.float32).astype(dtype).astype(np.float64)
    return np.moveaxis((codes * scale).reshape(v.shape), -1, axis)


WIDE = False


def mx_kscale(k):
    if not WIDE:
        return np.ones(k)
    levels = np.array([10, -10, 5, -5, 0])
    if k % 512:
        return np.exp2(np.random.permutation(np.resize(levels, k // 32))).repeat(32)
    a = np.empty((k // 512, 16))
    for p in range(k // 512):
        a[p, :8] = np.random.permutation(np.resize(levels, 8))
        for g in range(8):
            far = levels[np.abs(levels - a[p, g]) >= 10]
            a[p, g + 8] = far[np.random.randint(len(far))]
    return np.exp2(a.ravel()).repeat(32)


def f64(x):
    return np.asarray(x).astype(np.float64)


def striped(idx):
    return np.tile(idx.reshape(-1, 16).T, (8, 1)).astype(np.uint16)


def unstriped(offs):
    return offs[:16].T.reshape(-1).astype(np.int64)


E2M1 = np.array([0.0, 0.5, 1.0, 1.5, 2.0, 3.0, 4.0, 6.0, -0.0, -0.5, -1.0, -1.5, -2.0, -3.0, -4.0, -6.0])


def pack_weight(w, fmt):
    k, n = w.shape
    w = f64(np.asarray(w, np.float32).astype(ml_dtypes.bfloat16)).reshape(k // 32, 32, n)
    amax = np.abs(w).max(1)
    if fmt == "e4m3":
        byte = np.frexp(amax)[1] - 1 + 127 - 7
    else:
        mant, ex = np.frexp(amax / 6.0)
        byte = np.where(mant > 0.5, ex, ex - 1) + 127
    byte = np.clip(np.where(amax > 0, byte, 1), 1, 254)
    scaled = (w * np.exp2(127.0 - byte)[:, None, :]).reshape(k, n).astype(np.float32)
    by_word = np.ascontiguousarray(scaled.reshape(k // 512, 128, 4, n).transpose(0, 1, 3, 2))
    if fmt == "e4m3":
        words = by_word.astype(ml_dtypes.float8_e4m3fn).view(np.uint8)
    else:
        c = by_word.astype(ml_dtypes.float4_e2m1fn).view(np.uint8) & 0xF
        words = (c[..., 0::2] | (c[..., 1::2] << 4)).reshape(k // 512, 128, 2 * n)
    return np.ascontiguousarray(words), np.ascontiguousarray(byte.astype(np.uint8).reshape(k // 512, 16, n))


def unpack_weight(words, scales, fmt):
    g, _, n = scales.shape
    words = np.ascontiguousarray(words).reshape(g, 128, n, -1)
    if fmt == "e4m3":
        vals = words.view(ml_dtypes.float8_e4m3fn).astype(np.float64)
    else:
        nib = np.empty((g, 128, n, 4), np.uint8)
        nib[..., 0::2] = words & 0xF
        nib[..., 1::2] = words >> 4
        vals = E2M1[nib]
    vals = vals * np.repeat(np.exp2(scales.astype(np.float64) - 127.0), 8, axis=1)[..., None]
    return vals.transpose(0, 1, 3, 2).reshape(g * 512, n)


def gelu(v):
    return 0.5 * v * (1.0 + np.tanh(np.sqrt(2.0 / np.pi) * (v + 0.044715 * v**3)))


K, T, S, H, T2, P, N = 1024, 4096, 1024, 512, 2048, 512, 768

def setup_inputs():
    n = np.random.standard_normal
    s = mx_kscale(K)[:, None]
    u = mx_kscale(H)[:, None]
    perm = np.random.permutation(T2)
    tab_words, tab_scales = pack_weight(n((K, T)) * s, "e4m3")
    w2_words, w2_scales = pack_weight(2.0 * n((K, H)) / np.sqrt(K) / s, "e2m1")
    return {
        "tab_words": tab_words, "tab_scales": tab_scales,
        "offs": striped(np.random.permutation(T)[:S]),
        "offs2": striped(np.random.permutation(T2)[:S]),
        "offs3": striped(perm[:P]),
        "offs4": striped(perm[P:2 * P]),
        "w1": (0.6 * n((K, H)) / np.sqrt(K) / s).astype(np.float32),
        "w2_words": w2_words, "w2_scales": w2_scales,
        "gain": (np.exp(0.3 * n(H)) * u[:, 0]).astype(np.float32),
        "wgs": np.exp(0.3 * n((128, S))).astype(np.float32),
        "page0": (n((H, T2)) * u).astype(np.float32),
        "w3": (n((H, N)) / np.sqrt(H) / u).astype(np.float32),
        "base": (0.7 * n((N, T2))).astype(np.float32),
    }

def reference(tab_words, tab_scales, offs, offs2, offs3, offs4, w1, w2_words, w2_scales, gain, wgs, page0, w3, base):
    v = unpack_weight(tab_words, tab_scales, "e4m3")[:, unstriped(offs)]
    w2 = unpack_weight(w2_words, w2_scales, "e2m1")
    straight = mxq(f64(w1), 0, "e4m3").T @ v
    bent = np.tanh(w2.T @ v)
    h = f64(gain)[:, None] * (straight + bent)
    page = f64(page0).copy()
    page[:, unstriped(offs2)] = np.tile(f64(wgs), (H // 128, 1)) * h
    a = page[:, unstriped(offs3)]
    b = page[:, unstriped(offs4)]
    page[:, unstriped(offs3)] = a + b
    page[:, unstriped(offs4)] = a - b
    y = mxq(f64(w3), 0, "e4m3").T @ mxq(page, 0, "e4m3")
    return y + f64(base)

@@ -1,0 +1,279 @@
+from contextlib import ExitStack
+
+import concourse.mybir as mybir
+from concourse.masks import make_identity
+
+K, T, S, H, T2, PAIRS, N = 1024, 4096, 1024, 512, 2048, 512, 768
+FLOPS = 2 * (2 * K * H * S + H * N * T2)
+
+F32 = mybir.dt.float32
+BF16 = mybir.dt.bfloat16
+I32 = mybir.dt.int32
+U32 = mybir.dt.uint32
+U16 = mybir.dt.uint16
+U8 = mybir.dt.uint8
+FP8X4 = mybir.dt.float8_e4m3fn_x4
+FP4X4 = mybir.dt.float4_e2m1fn_x4
+ACT = mybir.ActivationFunctionType
+MULT = mybir.AluOpType.mult
+ADD = mybir.AluOpType.add
+
+P = 128
+PACK = 4
+PASSES = K // (P * PACK)
+BANK = 512
+HALVES = S // BANK
+BLOCKS = BANK // P
+CHUNKS = T2 // BANK
+N_PAIRS = N // (2 * P)
+
+
+def tile_list_donor_couple_exchange_kernel(
+    tc, tab_words, tab_scales, offs, offs2, offs3, offs4, w1, w2_words, w2_scales, gain, wgs, page0, w3, base, out
+):
+    nc = tc.nc
+    with ExitStack() as ctx:
+        keep = ctx.enter_context(tc.tile_pool(name="keep", bufs=1))
+        psum = ctx.enter_context(tc.psum_pool(name="psum", bufs=1))
+
+        def held(shape, dtype, name):
+            return keep.tile(shape, dtype, name=name, align_bytes=64)
+
+        def big(shape, name):
+            return keep.tile(shape, F32, name=name, tag="big", bufs=6, align_bytes=64)
+
+        list1 = keep.tile([P, S // 16], U16, name="list1")
+        list2 = keep.tile([P, S // 16], U16, name="list2")
+        list3 = keep.tile([P, PAIRS // 16], U16, name="list3")
+        list4 = keep.tile([P, PAIRS // 16], U16, name="list4")
+        nc.sync.dma_start(list1[:], offs)
+
+        tab_s = held([P, T], U8, "tab_s")
+        nc.vector.memset(tab_s[:].bitcast(I32), 0)
+        scale_rows = tab_scales.bitcast(I32).rearrange("a (q r) t -> r q a t", r=4)
+        for r in range(4):
+            nc.gpsimd.dma_start(tab_s[r:P:16, :].bitcast(I32), scale_rows[r])
+
+        w2_s = held([P, PASSES, H], U8, "w2_s")
+        nc.vector.memset(w2_s[:].bitcast(I32), 0)
+        for q in range(4):
+            nc.gpsimd.dma_start(
+                w2_s[32 * q : 32 * q + 4, :, :].bitcast(I32),
+                w2_scales.bitcast(I32)[:, 4 * q : 4 * q + 4, :].rearrange("a r c -> r a c"),
+            )
+        v_s1 = held([P, S], U8, "v_s1")
+        nc.vector.memset(v_s1[:].bitcast(I32), 0)
+        ident = held([P, P], F32, "ident")
+        make_identity(nc, ident[:])
+
+        tab_w = [held([P, T], I32, "tab_w%d" % a) for a in range(PASSES)]
+        for a in range(PASSES):
+            nc.sync.dma_start(tab_w[a][:], tab_words[a].rearrange("p t i -> p (t i)").bitcast(I32))
+        w2_w = held([P, PASSES, 2 * H], U8, "w2_w")
+        nc.sync.dma_start(w2_w[:].bitcast(I32), w2_words.bitcast(I32).rearrange("a p b -> p a b"))
+        w1_raw = [big([P, PACK, H], "w1_raw%d" % a) for a in range(PASSES)]
+        for a in range(PASSES):
+            nc.sync.dma_start(w1_raw[a][:], w1[512 * a : 512 * (a + 1), :].rearrange("(p i) r -> p i r", i=PACK))
+        gain_sb = held([P, PACK], F32, "gain_sb")
+        nc.sync.dma_start(gain_sb[:], gain.rearrange("(p t) -> p t", t=PACK))
+        nc.sync.dma_start(list2[:], offs2)
+
+        page = [held([P, T2], F32, "page%d" % t) for t in range(PACK)]
+        wgs_sb = [held([P, S], F32, "wgs%d" % t) for t in range(PACK)]
+        page_rows = page0.rearrange("(p t) c -> t p c", t=PACK)
+        wgs_rows = wgs.rearrange("(m t) j -> t m j", t=PACK)
+
+        def load_page(t):
+            for q in (0, 2, 1, 3):
+                nc.sync.dma_start(wgs_sb[t][32 * q : 32 * (q + 1), :], wgs_rows[t])
+            nc.sync.dma_start(page[t][:], page_rows[t])
+
+        load_page(0)
+        load_page(1)
+        nc.sync.dma_start(list3[:], offs3)
+        nc.sync.dma_start(list4[:], offs4)
+        load_page(2)
+        load_page(3)
+        w3_raw = held([P, PACK, N], F32, "w3_raw")
+        nc.sync.dma_start(w3_raw[:], w3.rearrange("(p i) n -> p i n", i=PACK))
+
+        v_s0 = held([P, S], U8, "v_s0")
+        nc.vector.tensor_copy(v_s0[:], tab_s[:].indirect(list1[:]))
+        for q in range(4):
+            nc.gpsimd.dma_start(
+                v_s1[32 * q : 32 * q + 4, :].bitcast(I32), v_s0[32 * q + 16 : 32 * q + 20, :].bitcast(I32)
+            )
+        v_s = [v_s0, v_s1]
+        v_w = {}
+        for a in range(PASSES):
+            for h in range(HALVES):
+                v_w[a, h] = held([P, BANK], U32, "v_w%d%d" % (a, h))
+                nc.vector.tensor_copy(
+                    v_w[a, h][:], tab_w[a][:].bitcast(U32).indirect(list1[:, 32 * h : 32 * (h + 1)])
+                )
+
+        def interleave(copy, dst, src):
+            copy(
+                dst[:].rearrange("p (c e) i -> p c i e", e=4),
+                src[:].rearrange("p i (c e) -> p c i e", e=4),
+            )
+
+        w1_w = [held([P, H], U32, "w1_w%d" % a) for a in range(PASSES)]
+        w1_s = [held([P, H], U8, "w1_s%d" % a) for a in range(PASSES)]
+        for a in range(PASSES):
+            w1_bf = held([P, H, PACK], BF16, "w1_bf%d" % a)
+            interleave(nc.vector.tensor_copy, w1_bf, w1_raw[a])
+            nc.vector.quantize_mx(
+                out=w1_w[a][:].bitcast(FP8X4), scales=w1_s[a][:], in_=w1_bf[:].rearrange("p c i -> p (c i)")
+            )
+
+        def product(h, b, rhs, rhs_scale):
+            acc = psum.tile([P, H], F32, name="acc", tag="mx", bufs=6)
+            for a in range(PASSES):
+                nc.tensor.matmul_mx(
+                    out=acc[:],
+                    lhsT=v_w[a, h][:, P * b : P * (b + 1)].bitcast(FP8X4),
+                    lhsT_scale=v_s[a][:, BANK * h + P * b : BANK * h + P * (b + 1)],
+                    rhs=rhs(a),
+                    rhs_scale=rhs_scale(a),
+                    start=(a == 0),
+                    stop=(a == PASSES - 1),
+                )
+            return acc[:].rearrange("j (m t) -> j t m", t=PACK)
+
+        bent = [big([P, BLOCKS, PACK, P], "bent%d" % h) for h in range(HALVES)]
+        straight = [big([P, BLOCKS, PACK, P], "straight%d" % h) for h in range(HALVES)]
+        for h in range(HALVES):
+            for b in range(BLOCKS):
+                acc = product(h, b, lambda a: w2_w[:, a, :].bitcast(FP4X4), lambda a: w2_s[:, a, :])
+                nc.scalar.activation(bent[h][:, b], acc, ACT.Tanh)
+
+        feat = {}
+
+        def make_straight(h):
+            for b in range(BLOCKS):
+                acc = product(h, b, lambda a: w1_w[a][:].bitcast(FP8X4), lambda a: w1_s[a][:])
+                nc.scalar.copy(straight[h][:, b], acc)
+
+        def make_features(t, h):
+            turned = psum.tile([P, BANK], F32, name="turned", tag="tr", bufs=2)
+            for b in range(BLOCKS):
+                cols = turned[:, P * b : P * (b + 1)]
+                nc.tensor.matmul(cols, bent[h][:, b, t, :], ident[:], start=True, stop=False, is_transpose=True)
+                nc.tensor.matmul(cols, straight[h][:, b, t, :], ident[:], start=False, stop=True, is_transpose=True)
+            feat[t, h] = held([P, BANK], F32, "feat%d%d" % (t, h))
+            nc.scalar.activation(feat[t, h][:], turned[:], ACT.Copy, scale=gain_sb[:, t : t + 1])
+
+        for h in range(HALVES):
+            make_straight(h)
+            make_features(0, h)
+            make_features(1, h)
+        for t in (2, 3):
+            for h in range(HALVES):
+                make_features(t, h)
+
+        scores = []
+        for k in range(CHUNKS * N_PAIRS // 2):
+            tile = big([P, 2, 2, BANK], "scores%d" % k)
+            scores.extend([tile[:, 0], tile[:, 1]])
+
+        def pair_rows(dram, u):
+            c, g = divmod(u, N_PAIRS)
+            return dram[2 * P * g : 2 * P * (g + 1), BANK * c : BANK * (c + 1)].rearrange("(n p) c -> p n c", p=P)
+
+        for u in range(CHUNKS * N_PAIRS):
+            nc.sync.dma_start(scores[u], pair_rows(base, u))
+
+        w3_bf = held([P, N, PACK], BF16, "w3_bf")
+        interleave(nc.scalar.copy, w3_bf, w3_raw)
+        w3_w = held([P, N], U32, "w3_w")
+        w3_s = held([P, N], U8, "w3_s")
+
+        def quantise_w3(lo, hi):
+            nc.vector.quantize_mx(
+                out=w3_w[:, lo:hi].bitcast(FP8X4),
+                scales=w3_s[:, lo:hi],
+                in_=w3_bf[:, lo:hi, :].rearrange("p c i -> p (c i)"),
+            )
+
+        page_bf = [held([P, BANK, PACK], BF16, "page_bf%d" % c) for c in range(CHUNKS)]
+        side_a, side_b, minus_b = {}, {}, {}
+
+        def put(t, h):
+            cols = slice(BANK * h, BANK * (h + 1))
+            nc.vector.tensor_tensor(
+                page[t][:].indirect(list2[:, 32 * h : 32 * (h + 1)]), feat[t, h][:], wgs_sb[t][:, cols], MULT
+            )
+
+        def fetch(t):
+            side_a[t] = keep.tile([P, PAIRS], F32, name="side_a", tag="side_a", bufs=2)
+            side_b[t] = keep.tile([P, PAIRS], F32, name="side_b", tag="side_b", bufs=2)
+            minus_b[t] = keep.tile([P, PAIRS], F32, name="minus_b", tag="minus_b", bufs=2)
+            nc.vector.tensor_copy(side_b[t][:], page[t][:].indirect(list4[:]))
+            nc.vector.tensor_copy(side_a[t][:], page[t][:].indirect(list3[:]))
+            nc.scalar.mul(minus_b[t][:], side_b[t][:], -1.0)
+
+        def put_sum(t):
+            nc.vector.tensor_tensor(page[t][:].indirect(list3[:]), side_a[t][:], side_b[t][:], ADD)
+
+        def put_difference(t):
+            nc.vector.tensor_tensor(page[t][:].indirect(list4[:]), side_a[t][:], minus_b[t][:], ADD)
+
+        def round_page(t):
+            for c in range(CHUNKS):
+                nc.scalar.copy(page_bf[c][:, :, t], page[t][:, BANK * c : BANK * (c + 1)])
+
+        put(0, 0)
+        put(1, 0)
+        put(0, 1)
+        put(1, 1)
+        fetch(0)
+        fetch(1)
+        put_sum(0)
+        put_sum(1)
+        put_difference(0)
+        round_page(0)
+        put(2, 0)
+        put_difference(1)
+        round_page(1)
+        put(2, 1)
+        put(3, 0)
+        fetch(2)
+        quantise_w3(0, 512)
+        put_sum(2)
+        put(3, 1)
+        put_difference(2)
+        fetch(3)
+        round_page(2)
+        quantise_w3(512, N)
+        put_sum(3)
+        put_difference(3)
+        round_page(3)
+
+        page_w = [held([P, BANK], U32, "page_w%d" % c) for c in range(CHUNKS)]
+        page_s = [held([P, BANK], U8, "page_s%d" % c) for c in range(CHUNKS)]
+
+        def quantise_page(c):
+            nc.vector.quantize_mx(
+                out=page_w[c][:].bitcast(FP8X4), scales=page_s[c][:], in_=page_bf[c][:].rearrange("p c i -> p (c i)")
+            )
+
+        quantise_page(0)
+        for u in range(CHUNKS * N_PAIRS):
+            c, g = divmod(u, N_PAIRS)
+            for n in range(2):
+                cols = slice(P * (2 * g + n), P * (2 * g + n + 1))
+                y = psum.tile([P, BANK], F32, name="y", tag="mx", bufs=6)
+                nc.tensor.matmul_mx(
+                    out=y[:],
+                    lhsT=w3_w[:, cols].bitcast(FP8X4),
+                    lhsT_scale=w3_s[:, cols],
+                    rhs=page_w[c][:].bitcast(FP8X4),
+                    rhs_scale=page_s[c][:],
+                    start=True,
+                    stop=True,
+                )
+                nc.vector.tensor_tensor(scores[u][:, n, :], y[:], scores[u][:, n, :], ADD)
+            nc.sync.dma_start(pair_rows(out, u), scores[u])
+            if g == 0 and c + 1 < CHUNKS:
+                quantise_page(c + 1)

@@ -46,172 +46,184 @@ def tile_list_donor_couple_exchange_kernel(
         list2 = keep.tile([P, S // 16], U16, name="list2")
         list3 = keep.tile([P, PAIRS // 16], U16, name="list3")
         list4 = keep.tile([P, PAIRS // 16], U16, name="list4")
-        nc.sync.dma_start(list1[:], offs)
-
-        tab_s = held([P, T], U8, "tab_s")
-        nc.vector.memset(tab_s[:].bitcast(I32), 0)
-        scale_rows = tab_scales.bitcast(I32).rearrange("a (q r) t -> r q a t", r=4)
-        for r in range(4):
-            nc.gpsimd.dma_start(tab_s[r:P:16, :].bitcast(I32), scale_rows[r])
-
+        tab_s = keep.tile([P, PASSES, T], U8, name="tab_s", tag="early_late", align_bytes=64)
+        nc.gpsimd.memset(tab_s[:, 0, :].bitcast(I32), 0)
+        nc.vector.memset(tab_s[:, 1, :].bitcast(I32), 0)
         w2_s = held([P, PASSES, H], U8, "w2_s")
         nc.vector.memset(w2_s[:].bitcast(I32), 0)
-        for q in range(4):
-            nc.gpsimd.dma_start(
-                w2_s[32 * q : 32 * q + 4, :, :].bitcast(I32),
-                w2_scales.bitcast(I32)[:, 4 * q : 4 * q + 4, :].rearrange("a r c -> r a c"),
-            )
-        v_s1 = held([P, S], U8, "v_s1")
-        nc.vector.memset(v_s1[:].bitcast(I32), 0)
         ident = held([P, P], F32, "ident")
         make_identity(nc, ident[:])
 
-        tab_w = [held([P, T], I32, "tab_w%d" % a) for a in range(PASSES)]
-        for a in range(PASSES):
-            nc.sync.dma_start(tab_w[a][:], tab_words[a].rearrange("p t i -> p (t i)").bitcast(I32))
-        w2_w = held([P, PASSES, 2 * H], U8, "w2_w")
-        nc.sync.dma_start(w2_w[:].bitcast(I32), w2_words.bitcast(I32).rearrange("a p b -> p a b"))
-        w1_raw = [big([P, PACK, H], "w1_raw%d" % a) for a in range(PASSES)]
-        for a in range(PASSES):
-            nc.sync.dma_start(w1_raw[a][:], w1[512 * a : 512 * (a + 1), :].rearrange("(p i) r -> p i r", i=PACK))
+        for tile, dram in ((list1, offs), (list2, offs2), (list3, offs3), (list4, offs4)):
+            nc.sync.dma_start(tile[:], dram)
         gain_sb = held([P, PACK], F32, "gain_sb")
         nc.sync.dma_start(gain_sb[:], gain.rearrange("(p t) -> p t", t=PACK))
-        nc.sync.dma_start(list2[:], offs2)
+        w2_w = held([P, PASSES, 2 * H], U8, "w2_w")
+        nc.sync.dma_start(w2_w[:].bitcast(I32), w2_words.bitcast(I32).rearrange("a p b -> p a b"))
+
+        def load_scale_rows(planes, dram):
+            for q in (0, 2, 1, 3):
+                nc.sync.dma_start(
+                    planes[32 * q : 32 * q + 4, :, :].bitcast(I32),
+                    dram.bitcast(I32)[:, 4 * q : 4 * q + 4, :].rearrange("a r c -> r a c"),
+                )
+
+        load_scale_rows(tab_s, tab_scales)
+        tab_w = [held([P, T], I32, "tab_w%d" % a) for a in range(PASSES)]
+        w1_pieces = ((0, slice(0, H)), (1, slice(0, H // 2)), (1, slice(H // 2, H)))
+        w1_first = big([P, PACK, H], "w1_first")
+        w1_second = big([P, 2, PACK, H // 2], "w1_second")
+        w1_raw = (w1_first[:], w1_second[:, 0], w1_second[:, 1])
+
+        def load_table(a):
+            nc.sync.dma_start(tab_w[a][:], tab_words[a].rearrange("p t i -> p (t i)").bitcast(I32))
+
+        def load_w1(piece):
+            a, cols = w1_pieces[piece]
+            nc.sync.dma_start(
+                w1_raw[piece], w1[512 * a : 512 * (a + 1), cols].rearrange("(p i) r -> p i r", i=PACK)
+            )
+
+        load_table(0)
+        load_scale_rows(w2_s, w2_scales)
+        load_table(1)
+        for piece in range(len(w1_pieces)):
+            load_w1(piece)
 
         page = [held([P, T2], F32, "page%d" % t) for t in range(PACK)]
         wgs_sb = [held([P, S], F32, "wgs%d" % t) for t in range(PACK)]
         page_rows = page0.rearrange("(p t) c -> t p c", t=PACK)
         wgs_rows = wgs.rearrange("(m t) j -> t m j", t=PACK)
 
-        def load_page(t):
+        def load_wgs(t):
             for q in (0, 2, 1, 3):
                 nc.sync.dma_start(wgs_sb[t][32 * q : 32 * (q + 1), :], wgs_rows[t])
+
+        def load_page(t):
             nc.sync.dma_start(page[t][:], page_rows[t])
 
-        load_page(0)
-        load_page(1)
-        nc.sync.dma_start(list3[:], offs3)
-        nc.sync.dma_start(list4[:], offs4)
-        load_page(2)
-        load_page(3)
-        w3_raw = held([P, PACK, N], F32, "w3_raw")
+        for t in range(PACK - 1):
+            load_wgs(t)
+            load_page(t)
+        w3_raw = keep.tile([P, PACK, N], F32, name="w3_raw", tag="early_late", align_bytes=64)
         nc.sync.dma_start(w3_raw[:], w3.rearrange("(p i) n -> p i n", i=PACK))
+        load_wgs(PACK - 1)
+        load_page(PACK - 1)
 
-        v_s0 = held([P, S], U8, "v_s0")
-        nc.vector.tensor_copy(v_s0[:], tab_s[:].indirect(list1[:]))
-        for q in range(4):
-            nc.gpsimd.dma_start(
-                v_s1[32 * q : 32 * q + 4, :].bitcast(I32), v_s0[32 * q + 16 : 32 * q + 20, :].bitcast(I32)
-            )
-        v_s = [v_s0, v_s1]
-        v_w = {}
+        v_s = [held([P, S], U8, "v_s%d" % a) for a in range(PASSES)]
         for a in range(PASSES):
-            for h in range(HALVES):
-                v_w[a, h] = held([P, BANK], U32, "v_w%d%d" % (a, h))
-                nc.vector.tensor_copy(
-                    v_w[a, h][:], tab_w[a][:].bitcast(U32).indirect(list1[:, 32 * h : 32 * (h + 1)])
-                )
+            nc.vector.tensor_copy(v_s[a][:], tab_s[:, a, :].indirect(list1[:]))
+        v_w = {}
+
+        def gather_words(a, h):
+            v_w[a, h] = held([P, BANK], U32, "v_w%d%d" % (a, h))
+            nc.vector.tensor_copy(v_w[a, h][:], tab_w[a][:].bitcast(U32).indirect(list1[:, 32 * h : 32 * (h + 1)]))
 
         def interleave(copy, dst, src):
             copy(
-                dst[:].rearrange("p (c e) i -> p c i e", e=4),
-                src[:].rearrange("p i (c e) -> p c i e", e=4),
+                dst.rearrange("p (c e) i -> p c i e", e=4),
+                src.rearrange("p i (c e) -> p c i e", e=4),
             )
 
         w1_w = [held([P, H], U32, "w1_w%d" % a) for a in range(PASSES)]
         w1_s = [held([P, H], U8, "w1_s%d" % a) for a in range(PASSES)]
-        for a in range(PASSES):
-            w1_bf = held([P, H, PACK], BF16, "w1_bf%d" % a)
-            interleave(nc.vector.tensor_copy, w1_bf, w1_raw[a])
+
+        def quantise_w1(piece):
+            a, cols = w1_pieces[piece]
+            w1_bf = held([P, cols.stop - cols.start, PACK], BF16, "w1_bf%d" % piece)
+            interleave(nc.vector.tensor_copy, w1_bf[:], w1_raw[piece])
             nc.vector.quantize_mx(
-                out=w1_w[a][:].bitcast(FP8X4), scales=w1_s[a][:], in_=w1_bf[:].rearrange("p c i -> p (c i)")
+                out=w1_w[a][:, cols].bitcast(FP8X4),
+                scales=w1_s[a][:, cols],
+                in_=w1_bf[:].rearrange("p c i -> p (c i)"),
             )
 
-        def product(h, b, rhs, rhs_scale):
-            acc = psum.tile([P, H], F32, name="acc", tag="mx", bufs=6)
-            for a in range(PASSES):
+        for a in range(PASSES):
+            for h in range(HALVES):
+                gather_words(a, h)
+        for piece in range(len(w1_pieces)):
+            quantise_w1(piece)
+
+        def product(h, b, passes):
+            acc = psum.tile([P, H], F32, name="acc", tag="bank", bufs=8)
+            for n, (a, cols, rhs, rhs_scale) in enumerate(passes):
                 nc.tensor.matmul_mx(
-                    out=acc[:],
+                    out=acc[:, cols],
                     lhsT=v_w[a, h][:, P * b : P * (b + 1)].bitcast(FP8X4),
                     lhsT_scale=v_s[a][:, BANK * h + P * b : BANK * h + P * (b + 1)],
-                    rhs=rhs(a),
-                    rhs_scale=rhs_scale(a),
-                    start=(a == 0),
-                    stop=(a == PASSES - 1),
+                    rhs=rhs,
+                    rhs_scale=rhs_scale,
+                    start=(n == 0),
+                    stop=(n == len(passes) - 1),
                 )
             return acc[:].rearrange("j (m t) -> j t m", t=PACK)
 
+        w2_passes = [(a, slice(0, H), w2_w[:, a, :].bitcast(FP4X4), w2_s[:, a, :]) for a in range(PASSES)]
+        w1_passes = [
+            (a, cols, w1_w[a][:, cols].bitcast(FP8X4), w1_s[a][:, cols])
+            for a, cols in w1_pieces
+        ]
+
         bent = [big([P, BLOCKS, PACK, P], "bent%d" % h) for h in range(HALVES)]
         straight = [big([P, BLOCKS, PACK, P], "straight%d" % h) for h in range(HALVES)]
-        for h in range(HALVES):
-            for b in range(BLOCKS):
-                acc = product(h, b, lambda a: w2_w[:, a, :].bitcast(FP4X4), lambda a: w2_s[:, a, :])
-                nc.scalar.activation(bent[h][:, b], acc, ACT.Tanh)
+        feat = [held([P, S], F32, "feat%d" % t) for t in range(PACK)]
 
-        feat = {}
+        def make_bent(h):
+            for b in range(BLOCKS):
+                nc.scalar.activation(bent[h][:, b], product(h, b, w2_passes), ACT.Tanh)
 
         def make_straight(h):
             for b in range(BLOCKS):
-                acc = product(h, b, lambda a: w1_w[a][:].bitcast(FP8X4), lambda a: w1_s[a][:])
-                nc.scalar.copy(straight[h][:, b], acc)
+                acc = product(h, b, w1_passes)
+                if h == 0 and b % 2 == 1:
+                    nc.vector.tensor_copy(straight[h][:, b], acc)
+                else:
+                    nc.scalar.copy(straight[h][:, b], acc)
 
         def make_features(t, h):
-            turned = psum.tile([P, BANK], F32, name="turned", tag="tr", bufs=2)
-            for b in range(BLOCKS):
-                cols = turned[:, P * b : P * (b + 1)]
-                nc.tensor.matmul(cols, bent[h][:, b, t, :], ident[:], start=True, stop=False, is_transpose=True)
-                nc.tensor.matmul(cols, straight[h][:, b, t, :], ident[:], start=False, stop=True, is_transpose=True)
-            feat[t, h] = held([P, BANK], F32, "feat%d%d" % (t, h))
-            nc.scalar.activation(feat[t, h][:], turned[:], ACT.Copy, scale=gain_sb[:, t : t + 1])
+            turned = psum.tile([P, BANK], F32, name="turned", tag="bank", bufs=8)
+            terms = [(term, b) for term in (bent, straight) for b in range(BLOCKS)]
+            for n, (term, b) in enumerate(terms):
+                nc.tensor.matmul(
+                    turned[:, P * b : P * (b + 1)],
+                    term[h][:, b, t, :],
+                    ident[:],
+                    start=(n == 0),
+                    stop=(n == len(terms) - 1),
+                    is_transpose=True,
+                )
+            nc.scalar.activation(feat[t][:, BANK * h : BANK * (h + 1)], turned[:], ACT.Copy, scale=gain_sb[:, t : t + 1])
 
+        make_bent(0)
+        make_bent(1)
         for h in range(HALVES):
             make_straight(h)
-            make_features(0, h)
-            make_features(1, h)
-        for t in (2, 3):
-            for h in range(HALVES):
+            for t in range(3):
                 make_features(t, h)
 
-        scores = []
-        for k in range(CHUNKS * N_PAIRS // 2):
-            tile = big([P, 2, 2, BANK], "scores%d" % k)
-            scores.extend([tile[:, 0], tile[:, 1]])
-
-        def pair_rows(dram, u):
-            c, g = divmod(u, N_PAIRS)
-            return dram[2 * P * g : 2 * P * (g + 1), BANK * c : BANK * (c + 1)].rearrange("(n p) c -> p n c", p=P)
-
-        for u in range(CHUNKS * N_PAIRS):
-            nc.sync.dma_start(scores[u], pair_rows(base, u))
-
-        w3_bf = held([P, N, PACK], BF16, "w3_bf")
-        interleave(nc.scalar.copy, w3_bf, w3_raw)
-        w3_w = held([P, N], U32, "w3_w")
-        w3_s = held([P, N], U8, "w3_s")
-
-        def quantise_w3(lo, hi):
-            nc.vector.quantize_mx(
-                out=w3_w[:, lo:hi].bitcast(FP8X4),
-                scales=w3_s[:, lo:hi],
-                in_=w3_bf[:, lo:hi, :].rearrange("p c i -> p (c i)"),
-            )
-
-        page_bf = [held([P, BANK, PACK], BF16, "page_bf%d" % c) for c in range(CHUNKS)]
+        chunks = [slice(0, 256), slice(256, 512)] + [slice(BANK * c, BANK * (c + 1)) for c in range(1, CHUNKS)]
+        page_bf = [held([P, cols.stop - cols.start, PACK], BF16, "page_bf%d" % cols.start) for cols in chunks]
         side_a, side_b, minus_b = {}, {}, {}
 
-        def put(t, h):
-            cols = slice(BANK * h, BANK * (h + 1))
+        def put(t, first, count):
+            cols = slice(first, first + count)
             nc.vector.tensor_tensor(
-                page[t][:].indirect(list2[:, 32 * h : 32 * (h + 1)]), feat[t, h][:], wgs_sb[t][:, cols], MULT
+                page[t][:].indirect(list2[:, first // 16 : (first + count) // 16]),
+                feat[t][:, cols],
+                wgs_sb[t][:, cols],
+                MULT,
             )
 
+        def side(name, t, shape, dtype):
+            return keep.tile(shape, dtype, name=name, tag="%s%d" % (name, t % 2), align_bytes=64)
+
         def fetch(t):
-            side_a[t] = keep.tile([P, PAIRS], F32, name="side_a", tag="side_a", bufs=2)
-            side_b[t] = keep.tile([P, PAIRS], F32, name="side_b", tag="side_b", bufs=2)
-            minus_b[t] = keep.tile([P, PAIRS], F32, name="minus_b", tag="minus_b", bufs=2)
+            side_a[t] = side("side_a", t, [P, PAIRS], F32)
+            side_b[t] = side("side_b", t, [P, PAIRS], F32)
+            minus_b[t] = side("minus_b", t, [P, PAIRS], F32)
             nc.vector.tensor_copy(side_b[t][:], page[t][:].indirect(list4[:]))
             nc.vector.tensor_copy(side_a[t][:], page[t][:].indirect(list3[:]))
-            nc.scalar.mul(minus_b[t][:], side_b[t][:], -1.0)
+            nc.vector.tensor_scalar(minus_b[t][:], side_b[t][:], -1.0, None, MULT)
 
         def put_sum(t):
             nc.vector.tensor_tensor(page[t][:].indirect(list3[:]), side_a[t][:], side_b[t][:], ADD)
@@ -220,60 +232,100 @@ def tile_list_donor_couple_exchange_kernel(
             nc.vector.tensor_tensor(page[t][:].indirect(list4[:]), side_a[t][:], minus_b[t][:], ADD)
 
         def round_page(t):
-            for c in range(CHUNKS):
-                nc.scalar.copy(page_bf[c][:, :, t], page[t][:, BANK * c : BANK * (c + 1)])
+            for tile, cols in zip(page_bf, chunks):
+                nc.scalar.copy(tile[:, :, t], page[t][:, cols])
 
-        put(0, 0)
-        put(1, 0)
-        put(0, 1)
-        put(1, 1)
+        put(0, 0, BANK)
+        put(1, 0, BANK)
+        put(2, 0, BANK)
+        put(0, BANK, BANK)
+        put(1, BANK, BANK)
         fetch(0)
         fetch(1)
+        for h in range(HALVES):
+            make_features(3, h)
+        w3_parts = (slice(0, 512), slice(512, N))
+        w3_bf = held([P, N, PACK], BF16, "w3_bf")
+        for n in range(N // P):
+            cols = slice(P * n, P * (n + 1))
+            interleave(nc.scalar.copy, w3_bf[:, cols, :], w3_raw[:, :, cols])
+
+        scores = []
+        for k in range(CHUNKS * N_PAIRS // 2):
+            tile = big([P, 2, 2, BANK], "scores%d" % k)
+            scores.extend([tile[:, 0], tile[:, 1]])
+
+        def rows(dram, first_row, count, cols):
+            return dram[first_row : first_row + count * P, cols].rearrange("(n p) c -> p n c", p=P)
+
+        for u in range(CHUNKS * N_PAIRS):
+            c, g = divmod(u, N_PAIRS)
+            nc.sync.dma_start(scores[u], rows(base, 2 * P * g, 2, slice(BANK * c, BANK * (c + 1))))
+
         put_sum(0)
         put_sum(1)
         put_difference(0)
-        round_page(0)
-        put(2, 0)
+        put(2, BANK, BANK)
         put_difference(1)
-        round_page(1)
-        put(2, 1)
-        put(3, 0)
         fetch(2)
-        quantise_w3(0, 512)
+        round_page(0)
+        round_page(1)
+        put(3, 0, S)
         put_sum(2)
-        put(3, 1)
-        put_difference(2)
         fetch(3)
-        round_page(2)
-        quantise_w3(512, N)
+        put_difference(2)
         put_sum(3)
+        round_page(2)
+        w3_w = side("side_b", 3, [P, N], U32)
+        w3_s = held([P, N], U8, "w3_s")
         put_difference(3)
+        for cols in w3_parts:
+            nc.vector.quantize_mx(
+                out=w3_w[:, cols].bitcast(FP8X4),
+                scales=w3_s[:, cols],
+                in_=w3_bf[:, cols, :].rearrange("p c i -> p (c i)"),
+            )
         round_page(3)
 
-        page_w = [held([P, BANK], U32, "page_w%d" % c) for c in range(CHUNKS)]
-        page_s = [held([P, BANK], U8, "page_s%d" % c) for c in range(CHUNKS)]
+        page_w = [held([P, cols.stop - cols.start], U32, "page_w%d" % cols.start) for cols in chunks]
+        page_s = [held([P, cols.stop - cols.start], U8, "page_s%d" % cols.start) for cols in chunks]
 
         def quantise_page(c):
             nc.vector.quantize_mx(
                 out=page_w[c][:].bitcast(FP8X4), scales=page_s[c][:], in_=page_bf[c][:].rearrange("p c i -> p (c i)")
             )
 
+        def read_out(y, n, c):
+            nc.tensor.matmul_mx(
+                out=y,
+                lhsT=w3_w[:, P * n : P * (n + 1)].bitcast(FP8X4),
+                lhsT_scale=w3_s[:, P * n : P * (n + 1)],
+                rhs=page_w[c][:].bitcast(FP8X4),
+                rhs_scale=page_s[c][:],
+                start=True,
+                stop=True,
+            )
+
         quantise_page(0)
-        for u in range(CHUNKS * N_PAIRS):
-            c, g = divmod(u, N_PAIRS)
-            for n in range(2):
-                cols = slice(P * (2 * g + n), P * (2 * g + n + 1))
-                y = psum.tile([P, BANK], F32, name="y", tag="mx", bufs=6)
-                nc.tensor.matmul_mx(
-                    out=y[:],
-                    lhsT=w3_w[:, cols].bitcast(FP8X4),
-                    lhsT_scale=w3_s[:, cols],
-                    rhs=page_w[c][:].bitcast(FP8X4),
-                    rhs_scale=page_s[c][:],
-                    start=True,
-                    stop=True,
-                )
-                nc.vector.tensor_tensor(scores[u][:, n, :], y[:], scores[u][:, n, :], ADD)
-            nc.sync.dma_start(pair_rows(out, u), scores[u])
-            if g == 0 and c + 1 < CHUNKS:
-                quantise_page(c + 1)
+        for c, cols in enumerate(chunks):
+            width = cols.stop - cols.start
+            inner = slice(cols.start % BANK, cols.start % BANK + width)
+            for g in range(N_PAIRS):
+                pair = scores[N_PAIRS * (cols.start // BANK) + g][:, :, inner]
+                last = c == len(chunks) - 1 and g == N_PAIRS - 1
+                if width < BANK:
+                    y = psum.tile([P, 2, width], F32, name="y", tag="bank", bufs=8)
+                    for n in range(2):
+                        read_out(y[:, n, :], 2 * g + n, c)
+                    nc.vector.tensor_tensor(pair, y[:], pair, ADD)
+                else:
+                    for n in range(2):
+                        y = psum.tile([P, width], F32, name="y", tag="bank", bufs=8)
+                        read_out(y[:], 2 * g + n, c)
+                        nc.vector.tensor_tensor(pair[:, n, :], y[:], pair[:, n, :], ADD)
+                        if last:
+                            nc.sync.dma_start(rows(out, P * (2 * g + n), 1, cols), pair[:, n : n + 1, :])
+                if not last:
+                    nc.sync.dma_start(rows(out, 2 * P * g, 2, cols), pair)
+                if g == 0 and c + 1 < len(chunks):
+                    quantise_page(c + 1)

@@ -91,24 +91,30 @@ def tile_list_donor_couple_exchange_kernel(
             load_w1(piece)
 
         page = [held([P, T2], F32, "page%d" % t) for t in range(PACK)]
-        wgs_sb = [held([P, S], F32, "wgs%d" % t) for t in range(PACK)]
         page_rows = page0.rearrange("(p t) c -> t p c", t=PACK)
-        wgs_rows = wgs.rearrange("(m t) j -> t m j", t=PACK)
+        wgs_rows = wgs.rearrange("(m t) j -> m t j", t=PACK)
+        weight = {}
 
-        def load_wgs(t):
+        def load_wgs(tiles, cols):
+            tile = held([P, len(tiles), cols.stop - cols.start], F32, "wgs%d_%d" % (tiles[0], cols.start))
             for q in (0, 2, 1, 3):
-                nc.sync.dma_start(wgs_sb[t][32 * q : 32 * (q + 1), :], wgs_rows[t])
+                nc.sync.dma_start(tile[32 * q : 32 * (q + 1)], wgs_rows[:, tiles[0] : tiles[-1] + 1, cols])
+            for n, t in enumerate(tiles):
+                weight[t, cols.start] = tile[:, n, :]
 
         def load_page(t):
             nc.sync.dma_start(page[t][:], page_rows[t])
 
-        for t in range(PACK - 1):
-            load_wgs(t)
-            load_page(t)
+        load_wgs([0], slice(0, BANK))
+        load_page(0)
+        load_wgs([1, 2], slice(0, BANK))
+        load_page(1)
+        load_page(2)
+        load_wgs([0, 1, 2], slice(BANK, S))
         w3_raw = keep.tile([P, PACK, N], F32, name="w3_raw", tag="early_late", align_bytes=64)
         nc.sync.dma_start(w3_raw[:], w3.rearrange("(p i) n -> p i n", i=PACK))
-        load_wgs(PACK - 1)
-        load_page(PACK - 1)
+        load_wgs([3], slice(0, S))
+        load_page(3)
 
         v_s = [held([P, S], U8, "v_s%d" % a) for a in range(PASSES)]
         for a in range(PASSES):
@@ -172,14 +178,6 @@ def tile_list_donor_couple_exchange_kernel(
             for b in range(BLOCKS):
                 nc.scalar.activation(bent[h][:, b], product(h, b, w2_passes), ACT.Tanh)
 
-        def make_straight(h):
-            for b in range(BLOCKS):
-                acc = product(h, b, w1_passes)
-                if h == 0 and b % 2 == 1:
-                    nc.vector.tensor_copy(straight[h][:, b], acc)
-                else:
-                    nc.scalar.copy(straight[h][:, b], acc)
-
         def make_features(t, h):
             turned = psum.tile([P, BANK], F32, name="turned", tag="bank", bufs=8)
             terms = [(term, b) for term in (bent, straight) for b in range(BLOCKS)]
@@ -196,10 +194,19 @@ def tile_list_donor_couple_exchange_kernel(
 
         make_bent(0)
         make_bent(1)
-        for h in range(HALVES):
-            make_straight(h)
-            for t in range(3):
-                make_features(t, h)
+        sums = [product(0, b, w1_passes) for b in range(BLOCKS)]
+        for b in range(BLOCKS):
+            copy = nc.vector.tensor_copy if b % 2 else nc.scalar.copy
+            copy(straight[0][:, b, 0, :], sums[b][:, 0, :])
+        make_features(0, 0)
+        for b in range(BLOCKS):
+            nc.scalar.copy(straight[0][:, b, 1:PACK, :], sums[b][:, 1:PACK, :])
+        make_features(1, 0)
+        make_features(2, 0)
+        for b in range(BLOCKS):
+            nc.scalar.copy(straight[1][:, b], product(1, b, w1_passes))
+        for t in range(3):
+            make_features(t, 1)
 
         chunks = [slice(0, 256), slice(256, 512)] + [slice(BANK * c, BANK * (c + 1)) for c in range(1, CHUNKS)]
         page_bf = [held([P, cols.stop - cols.start, PACK], BF16, "page_bf%d" % cols.start) for cols in chunks]
@@ -210,7 +217,7 @@ def tile_list_donor_couple_exchange_kernel(
             nc.vector.tensor_tensor(
                 page[t][:].indirect(list2[:, first // 16 : (first + count) // 16]),
                 feat[t][:, cols],
-                wgs_sb[t][:, cols],
+                weight[t, first],
                 MULT,
             )
 
@@ -223,7 +230,7 @@ def tile_list_donor_couple_exchange_kernel(
             minus_b[t] = side("minus_b", t, [P, PAIRS], F32)
             nc.vector.tensor_copy(side_b[t][:], page[t][:].indirect(list4[:]))
             nc.vector.tensor_copy(side_a[t][:], page[t][:].indirect(list3[:]))
-            nc.vector.tensor_scalar(minus_b[t][:], side_b[t][:], -1.0, None, MULT)
+            nc.gpsimd.tensor_scalar(minus_b[t][:], side_b[t][:], -1.0, 0.0, MULT, ADD)
 
         def put_sum(t):
             nc.vector.tensor_tensor(page[t][:].indirect(list3[:]), side_a[t][:], side_b[t][:], ADD)

@@ -62,11 +62,9 @@ def tile_list_donor_couple_exchange_kernel(
         nc.sync.dma_start(w2_w[:].bitcast(I32), w2_words.bitcast(I32).rearrange("a p b -> p a b"))
 
         def load_scale_rows(planes, dram):
-            for q in (0, 2, 1, 3):
-                nc.sync.dma_start(
-                    planes[32 * q : 32 * q + 4, :, :].bitcast(I32),
-                    dram.bitcast(I32)[:, 4 * q : 4 * q + 4, :].rearrange("a r c -> r a c"),
-                )
+            scale_rows = dram.bitcast(I32).rearrange("a (q r) c -> r q a c", r=4)
+            for r in range(4):
+                nc.sync.dma_start(planes[r:P:32, :, :].bitcast(I32), scale_rows[r])
 
         load_scale_rows(tab_s, tab_scales)
         tab_w = [held([P, T], I32, "tab_w%d" % a) for a in range(PASSES)]
@@ -113,7 +111,8 @@ def tile_list_donor_couple_exchange_kernel(
         load_wgs([0, 1, 2], slice(BANK, S))
         w3_raw = keep.tile([P, PACK, N], F32, name="w3_raw", tag="early_late", align_bytes=64)
         nc.sync.dma_start(w3_raw[:], w3.rearrange("(p i) n -> p i n", i=PACK))
-        load_wgs([3], slice(0, S))
+        load_wgs([3], slice(0, BANK))
+        load_wgs([3], slice(BANK, S))
         load_page(3)
 
         v_s = [held([P, S], U8, "v_s%d" % a) for a in range(PASSES)]
@@ -225,7 +224,10 @@ def tile_list_donor_couple_exchange_kernel(
             return keep.tile(shape, dtype, name=name, tag="%s%d" % (name, t % 2), align_bytes=64)
 
         def fetch(t):
-            side_a[t] = side("side_a", t, [P, PAIRS], F32)
+            if t == 2:
+                side_a[t] = keep.tile([P, PAIRS], F32, name="side_a", tag="wgs3_0", align_bytes=64)
+            else:
+                side_a[t] = side("side_a", t, [P, PAIRS], F32)
             side_b[t] = side("side_b", t, [P, PAIRS], F32)
             minus_b[t] = side("minus_b", t, [P, PAIRS], F32)
             nc.vector.tensor_copy(side_b[t][:], page[t][:].indirect(list4[:]))
@@ -274,16 +276,17 @@ def tile_list_donor_couple_exchange_kernel(
         put_difference(0)
         put(2, BANK, BANK)
         put_difference(1)
+        put(3, 0, BANK)
         fetch(2)
         round_page(0)
         round_page(1)
-        put(3, 0, S)
+        put(3, BANK, BANK)
         put_sum(2)
-        fetch(3)
         put_difference(2)
+        fetch(3)
         put_sum(3)
         round_page(2)
-        w3_w = side("side_b", 3, [P, N], U32)
+        w3_w = side("minus_b", 3, [P, N], U32)
         w3_s = held([P, N], U8, "w3_s")
         put_difference(3)
         for cols in w3_parts:
@@ -294,10 +297,12 @@ def tile_list_donor_couple_exchange_kernel(
             )
         round_page(3)
 
-        page_w = [held([P, cols.stop - cols.start], U32, "page_w%d" % cols.start) for cols in chunks]
-        page_s = [held([P, cols.stop - cols.start], U8, "page_s%d" % cols.start) for cols in chunks]
+        page_w, page_s = {}, {}
 
         def quantise_page(c):
+            width = chunks[c].stop - chunks[c].start
+            page_w[c] = keep.tile([P, width], U32, name="page_w", tag="page_w", bufs=2, align_bytes=64)
+            page_s[c] = keep.tile([P, width], U8, name="page_s", tag="page_s", bufs=2, align_bytes=64)
             nc.vector.quantize_mx(
                 out=page_w[c][:].bitcast(FP8X4), scales=page_s[c][:], in_=page_bf[c][:].rearrange("p c i -> p (c i)")
             )

@@ -20,12 +20,19 @@ ADD = mybir.AluOpType.add
 
 P = 128
 PACK = 4
-PASSES = K // (P * PACK)
+K_PASS = P * PACK
+PASSES = K // K_PASS
 BANK = 512
+BANKS = 8
 HALVES = S // BANK
 BLOCKS = BANK // P
-CHUNKS = T2 // BANK
+STRIPE = 16
+QUADRANT = 32
+SCALE_ROWS = 4
+LINE = 4
+BASE_CHUNKS = T2 // BANK
 N_PAIRS = N // (2 * P)
+BIG_SLOTS = 6
 
 
 def tile_list_donor_couple_exchange_kernel(
@@ -40,12 +47,12 @@ def tile_list_donor_couple_exchange_kernel(
             return keep.tile(shape, dtype, name=name, align_bytes=64)
 
         def big(shape, name):
-            return keep.tile(shape, F32, name=name, tag="big", bufs=6, align_bytes=64)
+            return keep.tile(shape, F32, name=name, tag="big", bufs=BIG_SLOTS, align_bytes=64)
 
-        list1 = keep.tile([P, S // 16], U16, name="list1")
-        list2 = keep.tile([P, S // 16], U16, name="list2")
-        list3 = keep.tile([P, PAIRS // 16], U16, name="list3")
-        list4 = keep.tile([P, PAIRS // 16], U16, name="list4")
+        list1 = keep.tile([P, S // STRIPE], U16, name="list1")
+        list2 = keep.tile([P, S // STRIPE], U16, name="list2")
+        list3 = keep.tile([P, PAIRS // STRIPE], U16, name="list3")
+        list4 = keep.tile([P, PAIRS // STRIPE], U16, name="list4")
         tab_s = keep.tile([P, PASSES, T], U8, name="tab_s", tag="early_late", align_bytes=64)
         nc.gpsimd.memset(tab_s[:, 0, :].bitcast(I32), 0)
         nc.vector.memset(tab_s[:, 1, :].bitcast(I32), 0)
@@ -54,17 +61,17 @@ def tile_list_donor_couple_exchange_kernel(
         ident = held([P, P], F32, "ident")
         make_identity(nc, ident[:])
 
-        for tile, dram in ((list1, offs), (list2, offs2), (list3, offs3), (list4, offs4)):
-            nc.sync.dma_start(tile[:], dram)
+        for list_tile, list_dram in ((list1, offs), (list2, offs2), (list3, offs3), (list4, offs4)):
+            nc.sync.dma_start(list_tile[:], list_dram)
         gain_sb = held([P, PACK], F32, "gain_sb")
         nc.sync.dma_start(gain_sb[:], gain.rearrange("(p t) -> p t", t=PACK))
         w2_w = held([P, PASSES, 2 * H], U8, "w2_w")
-        nc.sync.dma_start(w2_w[:].bitcast(I32), w2_words.bitcast(I32).rearrange("a p b -> p a b"))
+        nc.sync.dma_start(w2_w[:].bitcast(I32), w2_words.bitcast(I32).rearrange("a p col -> p a col"))
 
         def load_scale_rows(planes, dram):
-            scale_rows = dram.bitcast(I32).rearrange("a (q r) c -> r q a c", r=4)
-            for r in range(4):
-                nc.sync.dma_start(planes[r:P:32, :, :].bitcast(I32), scale_rows[r])
+            scale_rows = dram.bitcast(I32).rearrange("a (quadrant row) col -> row quadrant a col", row=SCALE_ROWS)
+            for row in range(SCALE_ROWS):
+                nc.sync.dma_start(planes[row:P:QUADRANT, :, :].bitcast(I32), scale_rows[row])
 
         load_scale_rows(tab_s, tab_scales)
         tab_w = [held([P, T], I32, "tab_w%d" % a) for a in range(PASSES)]
@@ -74,12 +81,12 @@ def tile_list_donor_couple_exchange_kernel(
         w1_raw = (w1_first[:], w1_second[:, 0], w1_second[:, 1])
 
         def load_table(a):
-            nc.sync.dma_start(tab_w[a][:], tab_words[a].rearrange("p t i -> p (t i)").bitcast(I32))
+            nc.sync.dma_start(tab_w[a][:], tab_words[a].rearrange("p col i -> p (col i)").bitcast(I32))
 
         def load_w1(piece):
             a, cols = w1_pieces[piece]
             nc.sync.dma_start(
-                w1_raw[piece], w1[512 * a : 512 * (a + 1), cols].rearrange("(p i) r -> p i r", i=PACK)
+                w1_raw[piece], w1[K_PASS * a : K_PASS * (a + 1), cols].rearrange("(p i) r -> p i r", i=PACK)
             )
 
         load_table(0)
@@ -89,30 +96,31 @@ def tile_list_donor_couple_exchange_kernel(
             load_w1(piece)
 
         page = [held([P, T2], F32, "page%d" % t) for t in range(PACK)]
-        page_rows = page0.rearrange("(p t) c -> t p c", t=PACK)
+        page_rows = page0.rearrange("(p t) col -> t p col", t=PACK)
         wgs_rows = wgs.rearrange("(m t) j -> m t j", t=PACK)
         weight = {}
 
-        def load_wgs(tiles, cols):
-            tile = held([P, len(tiles), cols.stop - cols.start], F32, "wgs%d_%d" % (tiles[0], cols.start))
-            for q in (0, 2, 1, 3):
-                nc.sync.dma_start(tile[32 * q : 32 * (q + 1)], wgs_rows[:, tiles[0] : tiles[-1] + 1, cols])
-            for n, t in enumerate(tiles):
-                weight[t, cols.start] = tile[:, n, :]
+        def load_wgs(page_tiles, h):
+            wgs_sb = held([P, len(page_tiles), BANK], F32, "wgs%d_%d" % (page_tiles[0], BANK * h))
+            src = wgs_rows[:, page_tiles[0] : page_tiles[-1] + 1, BANK * h : BANK * (h + 1)]
+            for quadrant in (0, 2, 1, 3):
+                nc.sync.dma_start(wgs_sb[QUADRANT * quadrant : QUADRANT * (quadrant + 1)], src)
+            for place, t in enumerate(page_tiles):
+                weight[t, h] = wgs_sb[:, place, :]
 
         def load_page(t):
             nc.sync.dma_start(page[t][:], page_rows[t])
 
-        load_wgs([0], slice(0, BANK))
+        load_wgs([0], 0)
         load_page(0)
-        load_wgs([1, 2], slice(0, BANK))
+        load_wgs([1, 2], 0)
         load_page(1)
         load_page(2)
-        load_wgs([0, 1, 2], slice(BANK, S))
+        load_wgs([0, 1, 2], 1)
         w3_raw = keep.tile([P, PACK, N], F32, name="w3_raw", tag="early_late", align_bytes=64)
-        nc.sync.dma_start(w3_raw[:], w3.rearrange("(p i) n -> p i n", i=PACK))
-        load_wgs([3], slice(0, BANK))
-        load_wgs([3], slice(BANK, S))
+        nc.sync.dma_start(w3_raw[:], w3.rearrange("(p i) col -> p i col", i=PACK))
+        load_wgs([3], 0)
+        load_wgs([3], 1)
         load_page(3)
 
         v_s = [held([P, S], U8, "v_s%d" % a) for a in range(PASSES)]
@@ -120,14 +128,17 @@ def tile_list_donor_couple_exchange_kernel(
             nc.vector.tensor_copy(v_s[a][:], tab_s[:, a, :].indirect(list1[:]))
         v_w = {}
 
+        def list_half(list_tile, h):
+            return list_tile[:, BANK // STRIPE * h : BANK // STRIPE * (h + 1)]
+
         def gather_words(a, h):
             v_w[a, h] = held([P, BANK], U32, "v_w%d%d" % (a, h))
-            nc.vector.tensor_copy(v_w[a, h][:], tab_w[a][:].bitcast(U32).indirect(list1[:, 32 * h : 32 * (h + 1)]))
+            nc.vector.tensor_copy(v_w[a, h][:], tab_w[a][:].bitcast(U32).indirect(list_half(list1, h)))
 
         def interleave(copy, dst, src):
             copy(
-                dst.rearrange("p (c e) i -> p c i e", e=4),
-                src.rearrange("p i (c e) -> p c i e", e=4),
+                dst.rearrange("p (run e) i -> p run i e", e=LINE),
+                src.rearrange("p i (run e) -> p run i e", e=LINE),
             )
 
         w1_w = [held([P, H], U32, "w1_w%d" % a) for a in range(PASSES)]
@@ -140,7 +151,7 @@ def tile_list_donor_couple_exchange_kernel(
             nc.vector.quantize_mx(
                 out=w1_w[a][:, cols].bitcast(FP8X4),
                 scales=w1_s[a][:, cols],
-                in_=w1_bf[:].rearrange("p c i -> p (c i)"),
+                in_=w1_bf[:].rearrange("p col i -> p (col i)"),
             )
 
         for a in range(PASSES):
@@ -150,24 +161,21 @@ def tile_list_donor_couple_exchange_kernel(
             quantise_w1(piece)
 
         def product(h, b, passes):
-            acc = psum.tile([P, H], F32, name="acc", tag="bank", bufs=8)
-            for n, (a, cols, rhs, rhs_scale) in enumerate(passes):
+            acc = psum.tile([P, H], F32, name="acc", tag="bank", bufs=BANKS)
+            for step, (a, cols, rhs, rhs_scale) in enumerate(passes):
                 nc.tensor.matmul_mx(
                     out=acc[:, cols],
                     lhsT=v_w[a, h][:, P * b : P * (b + 1)].bitcast(FP8X4),
                     lhsT_scale=v_s[a][:, BANK * h + P * b : BANK * h + P * (b + 1)],
                     rhs=rhs,
                     rhs_scale=rhs_scale,
-                    start=(n == 0),
-                    stop=(n == len(passes) - 1),
+                    start=(step == 0),
+                    stop=(step == len(passes) - 1),
                 )
             return acc[:].rearrange("j (m t) -> j t m", t=PACK)
 
         w2_passes = [(a, slice(0, H), w2_w[:, a, :].bitcast(FP4X4), w2_s[:, a, :]) for a in range(PASSES)]
-        w1_passes = [
-            (a, cols, w1_w[a][:, cols].bitcast(FP8X4), w1_s[a][:, cols])
-            for a, cols in w1_pieces
-        ]
+        w1_passes = [(a, cols, w1_w[a][:, cols].bitcast(FP8X4), w1_s[a][:, cols]) for a, cols in w1_pieces]
 
         bent = [big([P, BLOCKS, PACK, P], "bent%d" % h) for h in range(HALVES)]
         straight = [big([P, BLOCKS, PACK, P], "straight%d" % h) for h in range(HALVES)]
@@ -178,18 +186,19 @@ def tile_list_donor_couple_exchange_kernel(
                 nc.scalar.activation(bent[h][:, b], product(h, b, w2_passes), ACT.Tanh)
 
         def make_features(t, h):
-            turned = psum.tile([P, BANK], F32, name="turned", tag="bank", bufs=8)
+            turned = psum.tile([P, BANK], F32, name="turned", tag="bank", bufs=BANKS)
             terms = [(term, b) for term in (bent, straight) for b in range(BLOCKS)]
-            for n, (term, b) in enumerate(terms):
+            for step, (term, b) in enumerate(terms):
                 nc.tensor.matmul(
                     turned[:, P * b : P * (b + 1)],
                     term[h][:, b, t, :],
                     ident[:],
-                    start=(n == 0),
-                    stop=(n == len(terms) - 1),
+                    start=(step == 0),
+                    stop=(step == len(terms) - 1),
                     is_transpose=True,
                 )
-            nc.scalar.activation(feat[t][:, BANK * h : BANK * (h + 1)], turned[:], ACT.Copy, scale=gain_sb[:, t : t + 1])
+            half = feat[t][:, BANK * h : BANK * (h + 1)]
+            nc.scalar.activation(half, turned[:], ACT.Copy, scale=gain_sb[:, t : t + 1])
 
         make_bent(0)
         make_bent(1)
@@ -204,27 +213,24 @@ def tile_list_donor_couple_exchange_kernel(
         make_features(2, 0)
         for b in range(BLOCKS):
             nc.scalar.copy(straight[1][:, b], product(1, b, w1_passes))
-        for t in range(3):
+        for t in range(PACK - 1):
             make_features(t, 1)
 
-        chunks = [slice(0, 256), slice(256, 512)] + [slice(BANK * c, BANK * (c + 1)) for c in range(1, CHUNKS)]
+        chunks = [slice(0, BANK // 2), slice(BANK // 2, BANK)]
+        chunks = chunks + [slice(BANK * c, BANK * (c + 1)) for c in range(1, BASE_CHUNKS)]
         page_bf = [held([P, cols.stop - cols.start, PACK], BF16, "page_bf%d" % cols.start) for cols in chunks]
         side_a, side_b, minus_b = {}, {}, {}
 
-        def put(t, first, count):
-            cols = slice(first, first + count)
+        def put(t, h):
             nc.vector.tensor_tensor(
-                page[t][:].indirect(list2[:, first // 16 : (first + count) // 16]),
-                feat[t][:, cols],
-                weight[t, first],
-                MULT,
+                page[t][:].indirect(list_half(list2, h)), feat[t][:, BANK * h : BANK * (h + 1)], weight[t, h], MULT
             )
 
         def side(name, t, shape, dtype):
             return keep.tile(shape, dtype, name=name, tag="%s%d" % (name, t % 2), align_bytes=64)
 
         def fetch(t):
-            if t == 2:
+            if t == PACK - 2:
                 side_a[t] = keep.tile([P, PAIRS], F32, name="side_a", tag="wgs3_0", align_bytes=64)
             else:
                 side_a[t] = side("side_a", t, [P, PAIRS], F32)
@@ -232,7 +238,7 @@ def tile_list_donor_couple_exchange_kernel(
             minus_b[t] = side("minus_b", t, [P, PAIRS], F32)
             nc.vector.tensor_copy(side_b[t][:], page[t][:].indirect(list4[:]))
             nc.vector.tensor_copy(side_a[t][:], page[t][:].indirect(list3[:]))
-            nc.gpsimd.tensor_scalar(minus_b[t][:], side_b[t][:], -1.0, 0.0, MULT, ADD)
+            nc.scalar.mul(minus_b[t][:], side_b[t][:], -1.0)
 
         def put_sum(t):
             nc.vector.tensor_tensor(page[t][:].indirect(list3[:]), side_a[t][:], side_b[t][:], ADD)
@@ -241,18 +247,18 @@ def tile_list_donor_couple_exchange_kernel(
             nc.vector.tensor_tensor(page[t][:].indirect(list4[:]), side_a[t][:], minus_b[t][:], ADD)
 
         def round_page(t):
-            for tile, cols in zip(page_bf, chunks):
-                nc.scalar.copy(tile[:, :, t], page[t][:, cols])
+            for rounded, cols in zip(page_bf, chunks):
+                nc.scalar.copy(rounded[:, :, t], page[t][:, cols])
 
-        put(0, 0, BANK)
-        put(1, 0, BANK)
-        put(2, 0, BANK)
-        put(0, BANK, BANK)
-        put(1, BANK, BANK)
+        put(0, 0)
+        put(1, 0)
+        put(2, 0)
+        put(0, 1)
+        put(1, 1)
         fetch(0)
         fetch(1)
         for h in range(HALVES):
-            make_features(3, h)
+            make_features(PACK - 1, h)
         w3_parts = (slice(0, 512), slice(512, N))
         w3_bf = held([P, N, PACK], BF16, "w3_bf")
         for n in range(N // P):
@@ -260,27 +266,28 @@ def tile_list_donor_couple_exchange_kernel(
             interleave(nc.scalar.copy, w3_bf[:, cols, :], w3_raw[:, :, cols])
 
         scores = []
-        for k in range(CHUNKS * N_PAIRS // 2):
-            tile = big([P, 2, 2, BANK], "scores%d" % k)
-            scores.extend([tile[:, 0], tile[:, 1]])
+        for slot in range(BIG_SLOTS):
+            two_pairs = big([P, 2, 2, BANK], "scores%d" % slot)
+            scores.extend([two_pairs[:, 0], two_pairs[:, 1]])
 
         def rows(dram, first_row, count, cols):
-            return dram[first_row : first_row + count * P, cols].rearrange("(n p) c -> p n c", p=P)
+            return dram[first_row : first_row + count * P, cols].rearrange("(n p) col -> p n col", p=P)
 
-        for u in range(CHUNKS * N_PAIRS):
-            c, g = divmod(u, N_PAIRS)
-            nc.sync.dma_start(scores[u], rows(base, 2 * P * g, 2, slice(BANK * c, BANK * (c + 1))))
+        for base_chunk in range(BASE_CHUNKS):
+            for g in range(N_PAIRS):
+                cols = slice(BANK * base_chunk, BANK * (base_chunk + 1))
+                nc.sync.dma_start(scores[N_PAIRS * base_chunk + g], rows(base, 2 * P * g, 2, cols))
 
         put_sum(0)
         put_sum(1)
         put_difference(0)
-        put(2, BANK, BANK)
+        put(2, 1)
         put_difference(1)
-        put(3, 0, BANK)
+        put(3, 0)
         fetch(2)
         round_page(0)
         round_page(1)
-        put(3, BANK, BANK)
+        put(3, 1)
         put_sum(2)
         put_difference(2)
         fetch(3)
@@ -293,7 +300,7 @@ def tile_list_donor_couple_exchange_kernel(
             nc.vector.quantize_mx(
                 out=w3_w[:, cols].bitcast(FP8X4),
                 scales=w3_s[:, cols],
-                in_=w3_bf[:, cols, :].rearrange("p c i -> p (c i)"),
+                in_=w3_bf[:, cols, :].rearrange("p col i -> p (col i)"),
             )
         round_page(3)
 
@@ -304,7 +311,7 @@ def tile_list_donor_couple_exchange_kernel(
             page_w[c] = keep.tile([P, width], U32, name="page_w", tag="page_w", bufs=2, align_bytes=64)
             page_s[c] = keep.tile([P, width], U8, name="page_s", tag="page_s", bufs=2, align_bytes=64)
             nc.vector.quantize_mx(
-                out=page_w[c][:].bitcast(FP8X4), scales=page_s[c][:], in_=page_bf[c][:].rearrange("p c i -> p (c i)")
+                out=page_w[c][:].bitcast(FP8X4), scales=page_s[c][:], in_=page_bf[c][:].rearrange("p col i -> p (col i)")
             )
 
         def read_out(y, n, c):
@@ -326,17 +333,17 @@ def tile_list_donor_couple_exchange_kernel(
                 pair = scores[N_PAIRS * (cols.start // BANK) + g][:, :, inner]
                 last = c == len(chunks) - 1 and g == N_PAIRS - 1
                 if width < BANK:
-                    y = psum.tile([P, 2, width], F32, name="y", tag="bank", bufs=8)
-                    for n in range(2):
-                        read_out(y[:, n, :], 2 * g + n, c)
+                    y = psum.tile([P, 2, width], F32, name="y", tag="bank", bufs=BANKS)
+                    for member in range(2):
+                        read_out(y[:, member, :], 2 * g + member, c)
                     nc.vector.tensor_tensor(pair, y[:], pair, ADD)
                 else:
-                    for n in range(2):
-                        y = psum.tile([P, width], F32, name="y", tag="bank", bufs=8)
-                        read_out(y[:], 2 * g + n, c)
-                        nc.vector.tensor_tensor(pair[:, n, :], y[:], pair[:, n, :], ADD)
+                    for member in range(2):
+                        y = psum.tile([P, width], F32, name="y", tag="bank", bufs=BANKS)
+                        read_out(y[:], 2 * g + member, c)
+                        nc.vector.tensor_tensor(pair[:, member, :], y[:], pair[:, member, :], ADD)
                         if last:
-                            nc.sync.dma_start(rows(out, P * (2 * g + n), 1, cols), pair[:, n : n + 1, :])
+                            nc.sync.dma_start(rows(out, P * (2 * g + member), 1, cols), pair[:, member : member + 1, :])
                 if not last:
                     nc.sync.dma_start(rows(out, 2 * P * g, 2, cols), pair)
                 if g == 0 and c + 1 < len(chunks):

from contextlib import ExitStack

import concourse.mybir as mybir
from concourse.masks import make_identity

K, T, S, H, T2, PAIRS, N = 1024, 4096, 1024, 512, 2048, 512, 768
FLOPS = 2 * (2 * K * H * S + H * N * T2)

F32 = mybir.dt.float32
BF16 = mybir.dt.bfloat16
I32 = mybir.dt.int32
U32 = mybir.dt.uint32
U16 = mybir.dt.uint16
U8 = mybir.dt.uint8
FP8X4 = mybir.dt.float8_e4m3fn_x4
FP4X4 = mybir.dt.float4_e2m1fn_x4
ACT = mybir.ActivationFunctionType
MULT = mybir.AluOpType.mult
ADD = mybir.AluOpType.add

P = 128
PACK = 4
K_PASS = P * PACK
PASSES = K // K_PASS
BANK = 512
BANKS = 8
HALVES = S // BANK
BLOCKS = BANK // P
STRIPE = 16
QUADRANT = 32
SCALE_ROWS = 4
LINE = 4
BASE_CHUNKS = T2 // BANK
N_PAIRS = N // (2 * P)
BIG_SLOTS = 6


def tile_list_donor_couple_exchange_kernel(
    tc, tab_words, tab_scales, offs, offs2, offs3, offs4, w1, w2_words, w2_scales, gain, wgs, page0, w3, base, out
):
    nc = tc.nc
    with ExitStack() as ctx:
        keep = ctx.enter_context(tc.tile_pool(name="keep", bufs=1))
        psum = ctx.enter_context(tc.psum_pool(name="psum", bufs=1))

        def held(shape, dtype, name):
            return keep.tile(shape, dtype, name=name, align_bytes=64)

        def big(shape, name):
            return keep.tile(shape, F32, name=name, tag="big", bufs=BIG_SLOTS, align_bytes=64)

        list1 = keep.tile([P, S // STRIPE], U16, name="list1")
        list2 = keep.tile([P, S // STRIPE], U16, name="list2")
        list3 = keep.tile([P, PAIRS // STRIPE], U16, name="list3")
        list4 = keep.tile([P, PAIRS // STRIPE], U16, name="list4")
        tab_s = keep.tile([P, PASSES, T], U8, name="tab_s", tag="early_late", align_bytes=64)
        nc.gpsimd.memset(tab_s[:, 0, :].bitcast(I32), 0)
        nc.vector.memset(tab_s[:, 1, :].bitcast(I32), 0)
        w2_s = held([P, PASSES, H], U8, "w2_s")
        nc.vector.memset(w2_s[:].bitcast(I32), 0)
        ident = held([P, P], F32, "ident")
        make_identity(nc, ident[:])

        for list_tile, list_dram in ((list1, offs), (list2, offs2), (list3, offs3), (list4, offs4)):
            nc.sync.dma_start(list_tile[:], list_dram)
        gain_sb = held([P, PACK], F32, "gain_sb")
        nc.sync.dma_start(gain_sb[:], gain.rearrange("(p t) -> p t", t=PACK))
        w2_w = held([P, PASSES, 2 * H], U8, "w2_w")
        nc.sync.dma_start(w2_w[:].bitcast(I32), w2_words.bitcast(I32).rearrange("a p col -> p a col"))

        def load_scale_rows(planes, dram):
            scale_rows = dram.bitcast(I32).rearrange("a (quadrant row) col -> row quadrant a col", row=SCALE_ROWS)
            for row in range(SCALE_ROWS):
                nc.sync.dma_start(planes[row:P:QUADRANT, :, :].bitcast(I32), scale_rows[row])

        load_scale_rows(tab_s, tab_scales)
        tab_w = [held([P, T], I32, "tab_w%d" % a) for a in range(PASSES)]
        w1_pieces = ((0, slice(0, H)), (1, slice(0, H // 2)), (1, slice(H // 2, H)))
        w1_first = big([P, PACK, H], "w1_first")
        w1_second = big([P, 2, PACK, H // 2], "w1_second")
        w1_raw = (w1_first[:], w1_second[:, 0], w1_second[:, 1])

        def load_table(a):
            nc.sync.dma_start(tab_w[a][:], tab_words[a].rearrange("p col i -> p (col i)").bitcast(I32))

        def load_w1(piece):
            a, cols = w1_pieces[piece]
            nc.sync.dma_start(
                w1_raw[piece], w1[K_PASS * a : K_PASS * (a + 1), cols].rearrange("(p i) r -> p i r", i=PACK)
            )

        load_table(0)
        load_scale_rows(w2_s, w2_scales)
        load_table(1)
        for piece in range(len(w1_pieces)):
            load_w1(piece)

        page = [held([P, T2], F32, "page%d" % t) for t in range(PACK)]
        page_rows = page0.rearrange("(p t) col -> t p col", t=PACK)
        wgs_rows = wgs.rearrange("(m t) j -> m t j", t=PACK)
        weight = {}

        def load_wgs(page_tiles, h):
            wgs_sb = held([P, len(page_tiles), BANK], F32, "wgs%d_%d" % (page_tiles[0], BANK * h))
            src = wgs_rows[:, page_tiles[0] : page_tiles[-1] + 1, BANK * h : BANK * (h + 1)]
            for quadrant in (0, 2, 1, 3):
                nc.sync.dma_start(wgs_sb[QUADRANT * quadrant : QUADRANT * (quadrant + 1)], src)
            for place, t in enumerate(page_tiles):
                weight[t, h] = wgs_sb[:, place, :]

        def load_page(t):
            nc.sync.dma_start(page[t][:], page_rows[t])

        load_wgs([0], 0)
        load_page(0)
        load_wgs([1, 2], 0)
        load_page(1)
        load_page(2)
        load_wgs([0, 1, 2], 1)
        w3_raw = keep.tile([P, PACK, N], F32, name="w3_raw", tag="early_late", align_bytes=64)
        nc.sync.dma_start(w3_raw[:], w3.rearrange("(p i) col -> p i col", i=PACK))
        load_wgs([3], 0)
        load_wgs([3], 1)
        load_page(3)

        v_s = [held([P, S], U8, "v_s%d" % a) for a in range(PASSES)]
        for a in range(PASSES):
            nc.vector.tensor_copy(v_s[a][:], tab_s[:, a, :].indirect(list1[:]))
        v_w = {}

        def list_half(list_tile, h):
            return list_tile[:, BANK // STRIPE * h : BANK // STRIPE * (h + 1)]

        def gather_words(a, h):
            v_w[a, h] = held([P, BANK], U32, "v_w%d%d" % (a, h))
            nc.vector.tensor_copy(v_w[a, h][:], tab_w[a][:].bitcast(U32).indirect(list_half(list1, h)))

        def interleave(copy, dst, src):
            copy(
                dst.rearrange("p (run e) i -> p run i e", e=LINE),
                src.rearrange("p i (run e) -> p run i e", e=LINE),
            )

        w1_w = [held([P, H], U32, "w1_w%d" % a) for a in range(PASSES)]
        w1_s = [held([P, H], U8, "w1_s%d" % a) for a in range(PASSES)]

        def quantise_w1(piece):
            a, cols = w1_pieces[piece]
            w1_bf = held([P, cols.stop - cols.start, PACK], BF16, "w1_bf%d" % piece)
            interleave(nc.vector.tensor_copy, w1_bf[:], w1_raw[piece])
            nc.vector.quantize_mx(
                out=w1_w[a][:, cols].bitcast(FP8X4),
                scales=w1_s[a][:, cols],
                in_=w1_bf[:].rearrange("p col i -> p (col i)"),
            )

        for a in range(PASSES):
            for h in range(HALVES):
                gather_words(a, h)
        for piece in range(len(w1_pieces)):
            quantise_w1(piece)

        def product(h, b, passes):
            acc = psum.tile([P, H], F32, name="acc", tag="bank", bufs=BANKS)
            for step, (a, cols, rhs, rhs_scale) in enumerate(passes):
                nc.tensor.matmul_mx(
                    out=acc[:, cols],
                    lhsT=v_w[a, h][:, P * b : P * (b + 1)].bitcast(FP8X4),
                    lhsT_scale=v_s[a][:, BANK * h + P * b : BANK * h + P * (b + 1)],
                    rhs=rhs,
                    rhs_scale=rhs_scale,
                    start=(step == 0),
                    stop=(step == len(passes) - 1),
                )
            return acc[:].rearrange("j (m t) -> j t m", t=PACK)

        w2_passes = [(a, slice(0, H), w2_w[:, a, :].bitcast(FP4X4), w2_s[:, a, :]) for a in range(PASSES)]
        w1_passes = [(a, cols, w1_w[a][:, cols].bitcast(FP8X4), w1_s[a][:, cols]) for a, cols in w1_pieces]

        bent = [big([P, BLOCKS, PACK, P], "bent%d" % h) for h in range(HALVES)]
        straight = [big([P, BLOCKS, PACK, P], "straight%d" % h) for h in range(HALVES)]
        feat = [held([P, S], F32, "feat%d" % t) for t in range(PACK)]

        def make_bent(h):
            for b in range(BLOCKS):
                nc.scalar.activation(bent[h][:, b], product(h, b, w2_passes), ACT.Tanh)

        def make_features(t, h):
            turned = psum.tile([P, BANK], F32, name="turned", tag="bank", bufs=BANKS)
            terms = [(term, b) for term in (bent, straight) for b in range(BLOCKS)]
            for step, (term, b) in enumerate(terms):
                nc.tensor.matmul(
                    turned[:, P * b : P * (b + 1)],
                    term[h][:, b, t, :],
                    ident[:],
                    start=(step == 0),
                    stop=(step == len(terms) - 1),
                    is_transpose=True,
                )
            half = feat[t][:, BANK * h : BANK * (h + 1)]
            nc.scalar.activation(half, turned[:], ACT.Copy, scale=gain_sb[:, t : t + 1])

        make_bent(0)
        make_bent(1)
        sums = [product(0, b, w1_passes) for b in range(BLOCKS)]
        for b in range(BLOCKS):
            copy = nc.vector.tensor_copy if b % 2 else nc.scalar.copy
            copy(straight[0][:, b, 0, :], sums[b][:, 0, :])
        make_features(0, 0)
        for b in range(BLOCKS):
            nc.scalar.copy(straight[0][:, b, 1:PACK, :], sums[b][:, 1:PACK, :])
        make_features(1, 0)
        make_features(2, 0)
        for b in range(BLOCKS):
            nc.scalar.copy(straight[1][:, b], product(1, b, w1_passes))
        for t in range(PACK - 1):
            make_features(t, 1)

        chunks = [slice(0, BANK // 2), slice(BANK // 2, BANK)]
        chunks = chunks + [slice(BANK * c, BANK * (c + 1)) for c in range(1, BASE_CHUNKS)]
        page_bf = [held([P, cols.stop - cols.start, PACK], BF16, "page_bf%d" % cols.start) for cols in chunks]
        side_a, side_b, minus_b = {}, {}, {}

        def put(t, h):
            nc.vector.tensor_tensor(
                page[t][:].indirect(list_half(list2, h)), feat[t][:, BANK * h : BANK * (h + 1)], weight[t, h], MULT
            )

        def side(name, t, shape, dtype):
            return keep.tile(shape, dtype, name=name, tag="%s%d" % (name, t % 2), align_bytes=64)

        def fetch(t):
            if t == PACK - 2:
                side_a[t] = keep.tile([P, PAIRS], F32, name="side_a", tag="wgs3_0", align_bytes=64)
            else:
                side_a[t] = side("side_a", t, [P, PAIRS], F32)
            side_b[t] = side("side_b", t, [P, PAIRS], F32)
            minus_b[t] = side("minus_b", t, [P, PAIRS], F32)
            nc.vector.tensor_copy(side_b[t][:], page[t][:].indirect(list4[:]))
            nc.vector.tensor_copy(side_a[t][:], page[t][:].indirect(list3[:]))
            nc.scalar.mul(minus_b[t][:], side_b[t][:], -1.0)

        def put_sum(t):
            nc.vector.tensor_tensor(page[t][:].indirect(list3[:]), side_a[t][:], side_b[t][:], ADD)

        def put_difference(t):
            nc.vector.tensor_tensor(page[t][:].indirect(list4[:]), side_a[t][:], minus_b[t][:], ADD)

        def round_page(t):
            for rounded, cols in zip(page_bf, chunks):
                nc.scalar.copy(rounded[:, :, t], page[t][:, cols])

        put(0, 0)
        put(1, 0)
        put(2, 0)
        put(0, 1)
        put(1, 1)
        fetch(0)
        fetch(1)
        for h in range(HALVES):
            make_features(PACK - 1, h)
        w3_parts = (slice(0, 512), slice(512, N))
        w3_bf = held([P, N, PACK], BF16, "w3_bf")
        for n in range(N // P):
            cols = slice(P * n, P * (n + 1))
            interleave(nc.scalar.copy, w3_bf[:, cols, :], w3_raw[:, :, cols])

        scores = []
        for slot in range(BIG_SLOTS):
            two_pairs = big([P, 2, 2, BANK], "scores%d" % slot)
            scores.extend([two_pairs[:, 0], two_pairs[:, 1]])

        def rows(dram, first_row, count, cols):
            return dram[first_row : first_row + count * P, cols].rearrange("(n p) col -> p n col", p=P)

        for base_chunk in range(BASE_CHUNKS):
            for g in range(N_PAIRS):
                cols = slice(BANK * base_chunk, BANK * (base_chunk + 1))
                nc.sync.dma_start(scores[N_PAIRS * base_chunk + g], rows(base, 2 * P * g, 2, cols))

        put_sum(0)
        put_sum(1)
        put_difference(0)
        put(2, 1)
        put_difference(1)
        put(3, 0)
        fetch(2)
        round_page(0)
        round_page(1)
        put(3, 1)
        put_sum(2)
        put_difference(2)
        fetch(3)
        put_sum(3)
        round_page(2)
        w3_w = side("minus_b", 3, [P, N], U32)
        w3_s = held([P, N], U8, "w3_s")
        put_difference(3)
        for cols in w3_parts:
            nc.vector.quantize_mx(
                out=w3_w[:, cols].bitcast(FP8X4),
                scales=w3_s[:, cols],
                in_=w3_bf[:, cols, :].rearrange("p col i -> p (col i)"),
            )
        round_page(3)

        page_w, page_s = {}, {}

        def quantise_page(c):
            width = chunks[c].stop - chunks[c].start
            page_w[c] = keep.tile([P, width], U32, name="page_w", tag="page_w", bufs=2, align_bytes=64)
            page_s[c] = keep.tile([P, width], U8, name="page_s", tag="page_s", bufs=2, align_bytes=64)
            nc.vector.quantize_mx(
                out=page_w[c][:].bitcast(FP8X4), scales=page_s[c][:], in_=page_bf[c][:].rearrange("p col i -> p (col i)")
            )

        def read_out(y, n, c):
            nc.tensor.matmul_mx(
                out=y,
                lhsT=w3_w[:, P * n : P * (n + 1)].bitcast(FP8X4),
                lhsT_scale=w3_s[:, P * n : P * (n + 1)],
                rhs=page_w[c][:].bitcast(FP8X4),
                rhs_scale=page_s[c][:],
                start=True,
                stop=True,
            )

        quantise_page(0)
        for c, cols in enumerate(chunks):
            width = cols.stop - cols.start
            inner = slice(cols.start % BANK, cols.start % BANK + width)
            for g in range(N_PAIRS):
                pair = scores[N_PAIRS * (cols.start // BANK) + g][:, :, inner]
                last = c == len(chunks) - 1 and g == N_PAIRS - 1
                if width < BANK:
                    y = psum.tile([P, 2, width], F32, name="y", tag="bank", bufs=BANKS)
                    for member in range(2):
                        read_out(y[:, member, :], 2 * g + member, c)
                    nc.vector.tensor_tensor(pair, y[:], pair, ADD)
                else:
                    for member in range(2):
                        y = psum.tile([P, width], F32, name="y", tag="bank", bufs=BANKS)
                        read_out(y[:], 2 * g + member, c)
                        nc.vector.tensor_tensor(pair[:, member, :], y[:], pair[:, member, :], ADD)
                        if last:
                            nc.sync.dma_start(rows(out, P * (2 * g + member), 1, cols), pair[:, member : member + 1, :])
                if not last:
                    nc.sync.dma_start(rows(out, 2 * P * g, 2, cols), pair)
                if g == 0 and c + 1 < len(chunks):
                    quantise_page(c + 1)
